import numpy as np
import ml_dtypes


def mxq(x, axis, fmt="e4m3"):
    dtype, down = {"e4m3": (ml_dtypes.float8_e4m3fn, 7), "e5m2": (ml_dtypes.float8_e5m2, 14)}[fmt]
    v = np.moveaxis(np.asarray(x, np.float32).astype(ml_dtypes.bfloat16).astype(np.float64), axis, -1)
    blocks = v.reshape(v.shape[:-1] + (-1, 32))
    amax = np.abs(blocks).max(-1, keepdims=True)
    byte = np.maximum(np.where(amax > 0, np.frexp(amax)[1] - 1 + 127, 0) - down, 1)
    scale = np.exp2(byte - 127.0)
    codes = (blocks / scale).astype(np.float32).astype(dtype).astype(np.float64)
    return np.moveaxis((codes * scale).reshape(v.shape), -1, axis)


WIDE = False


def mx_kscale(k):
    if not WIDE:
        return np.ones(k)
    levels = np.array([10, -10, 5, -5, 0])
    if k % 512:
        return np.exp2(np.random.permutation(np.resize(levels, k // 32))).repeat(32)
    a = np.empty((k // 512, 16))
    for p in range(k // 512):
        a[p, :8] = np.random.permutation(np.resize(levels, 8))
        for g in range(8):
            far = levels[np.abs(levels - a[p, g]) >= 10]
            a[p, g + 8] = far[np.random.randint(len(far))]
    return np.exp2(a.ravel()).repeat(32)


def f64(x):
    return np.asarray(x).astype(np.float64)


def striped(idx):
    return np.tile(idx.reshape(-1, 16).T, (8, 1)).astype(np.uint16)


def unstriped(offs):
    return offs[:16].T.reshape(-1).astype(np.int64)


def striped8(idx):
    return np.concatenate([x.reshape(-1, 16).T for x in idx]).astype(np.uint16)


def runs(offs, k):
    lists = np.stack([offs[16 * r : 16 * r + 16].T.reshape(-1) for r in range(8)]).astype(np.int64)
    return lists[np.arange(k) % 512 // 64]


def pack_weight(w):
    k, n = w.shape
    w = f64(np.asarray(w, np.float32).astype(ml_dtypes.bfloat16)).reshape(k // 32, 32, n)
    amax = np.abs(w).max(1)
    byte = np.clip(np.where(amax > 0, np.frexp(amax)[1] - 1 + 127 - 7, 1), 1, 254)
    scaled = (w * np.exp2(127.0 - byte)[:, None, :]).reshape(k, n).astype(np.float32)
    words = np.ascontiguousarray(scaled.reshape(k // 512, 128, 4, n).transpose(0, 1, 3, 2)).astype(ml_dtypes.float8_e4m3fn).view(np.uint8)
    return words, np.ascontiguousarray(byte.astype(np.uint8).reshape(k // 512, 16, n))


def unpack_weight(words, scales):
    g, p, n, _ = words.shape
    vals = np.ascontiguousarray(words).view(ml_dtypes.float8_e4m3fn).astype(np.float64) * np.repeat(np.exp2(scales.astype(np.float64) - 127.0), 8, axis=1)[..., None]
    return vals.transpose(0, 1, 3, 2).reshape(g * 512, n)


K, T, S, H, W, G = 512, 2048, 256, 512, 128, 2048


def setup_inputs():
    n = np.random.standard_normal
    s = mx_kscale(K)[:, None]
    packed_xT = pack_weight(n((K, T)) * s)
    packed_dT = pack_weight(n((K, G)) / s)
    perm = np.random.permutation(S)
    return {
        "x_words": packed_xT[0],
        "x_scales": packed_xT[1],
        "w1": (n((K, H)) / np.sqrt(K) / s).astype(np.float32),
        "gs": (np.random.uniform(0.5, 1.5, (K, 1)) * s).astype(np.float32),
        "d_words": packed_dT[0],
        "d_scales": packed_dT[1],
        "offs": striped(np.random.permutation(T)[:S]),
        "n1": striped(perm[:W]),
        "n2": striped(perm[W:]),
        "n3": striped(np.random.permutation(S)),
        "k1": striped8(np.random.randint(0, G, (8, H))),
        "n4": striped8(np.stack([np.random.permutation(S) for _ in range(8)])),
    }


def reference(x_words, x_scales, w1, gs, d_words, d_scales, offs, n1, n2, n3, k1, n4):
    d_k1 = unpack_weight(d_words, d_scales)[np.arange(K)[:, None], runs(k1, K)]
    xq = unpack_weight(x_words, x_scales)[:, unstriped(offs)]
    y = mxq(f64(w1), 0, "e4m3").T @ xq
    pa = y[:, unstriped(n1)]
    pb = y[:, unstriped(n2)]
    rb = np.minimum(pa, pb)
    ra = np.maximum(pa, pb)
    ds = np.zeros((H, S))
    ds[:, unstriped(n1)] = ra
    dt = ds.copy()
    dt[:, unstriped(n2)] = rb
    z = f64(gs) * (dt - dt[:, unstriped(n3)])
    h = 0.0625 * ((d_k1.T @ mxq(z, 0, "e4m3")))
    return h / (np.abs(h[np.arange(H)[:, None], runs(n4, H)]) + 0.5)

@@ -1,0 +1,229 @@
+from contextlib import ExitStack
+
+import concourse.mybir as mybir
+
+K, T, S, H, W, G = 512, 2048, 256, 512, 128, 2048
+FLOPS = 2 * K * H * S + 2 * K * H * S
+
+F32 = mybir.dt.float32
+BF16 = mybir.dt.bfloat16
+I32 = mybir.dt.int32
+U32 = mybir.dt.uint32
+U16 = mybir.dt.uint16
+U8 = mybir.dt.uint8
+FP8X4 = mybir.dt.float8_e4m3fn_x4
+ALU = mybir.AluOpType
+ACT = mybir.ActivationFunctionType
+
+P = 128
+PACK = 4
+HALF = S // 2
+
+
+def tile_picked_denseorddnorm_none_p_kernel(
+    tc, x_words, x_scales, w1, gs, d_words, d_scales, offs, n1, n2, n3, k1, n4, out
+):
+    nc = tc.nc
+    with ExitStack() as ctx:
+        lists = ctx.enter_context(tc.tile_pool(name="lists", bufs=1))
+        sb = ctx.enter_context(tc.tile_pool(name="sb", bufs=1))
+        psum = ctx.enter_context(tc.psum_pool(name="psum", bufs=4))
+
+        offs_t = lists.tile([P, S // 16], U16, name="offs_t")
+        n1_t = lists.tile([P, W // 16], U16, name="n1_t")
+        n2_t = lists.tile([P, W // 16], U16, name="n2_t")
+        n3_t = lists.tile([P, S // 16], U16, name="n3_t")
+        k1_t = lists.tile([P, H // 16], U16, name="k1_t")
+        n4_t = lists.tile([P, S // 16], U16, name="n4_t")
+
+        x_table = sb.tile([P, T], I32, name="x_table", align_bytes=64)
+        xs_table = sb.tile([P, T], U8, name="xs_table", tag="xs", align_bytes=64)
+        d_table = sb.tile([P, G], I32, name="d_table", align_bytes=64)
+        ds_table = sb.tile([P, G], U8, name="ds_table", align_bytes=64)
+        w_raw = sb.tile([P, PACK, H], F32, name="w_raw", align_bytes=64)
+        gs_t = sb.tile([P, PACK], F32, name="gs_t")
+        eight = sb.tile([P, 1], F32, name="eight")
+        d_plane = sb.tile([P, H], U8, name="d_plane", align_bytes=64)
+
+        nc.vector.memset(xs_table[:].bitcast(I32), 0)
+        for q in range(4):
+            nc.gpsimd.dma_start(
+                xs_table[32 * q : 32 * q + 4, :].bitcast(I32), x_scales[0, 4 * q : 4 * q + 4, :].bitcast(I32)
+            )
+        nc.vector.memset(ds_table[:].bitcast(I32), 0)
+        nc.vector.memset(d_plane[:].bitcast(I32), 0)
+        nc.vector.memset(eight[:], 8.0)
+
+        nc.sync.dma_start(offs_t[:], offs)
+        nc.sync.dma_start(w_raw[:], w1.rearrange("(p j) c -> p j c", j=PACK))
+        nc.sync.dma_start(x_table[:], x_words[0].rearrange("p n t -> p (n t)").bitcast(I32))
+        nc.sync.dma_start(n1_t[:], n1)
+        nc.sync.dma_start(n2_t[:], n2)
+        nc.sync.dma_start(k1_t[:], k1)
+        nc.sync.dma_start(ds_table[0:P:8, :].bitcast(I32), d_scales[0].bitcast(I32))
+        nc.sync.dma_start(gs_t[:], gs.rearrange("(p t) o -> p (t o)", t=PACK))
+        nc.sync.dma_start(d_table[:], d_words[0].rearrange("p n t -> p (n t)").bitcast(I32))
+        nc.sync.dma_start(n3_t[:], n3)
+        nc.sync.dma_start(n4_t[:], n4)
+
+        w_by_slot = w_raw[:].rearrange("p j (m t) -> p m t j", t=PACK)
+        w_bf_a = sb.tile([P, 2 * P * PACK], BF16, name="w_bf_a", align_bytes=64)
+        w_bf_b = sb.tile([P, 2 * P * PACK], BF16, name="w_bf_b", align_bytes=64)
+        nc.vector.tensor_copy(w_bf_a[:].rearrange("p (t m j) -> p m t j", t=2, j=PACK), w_by_slot[:, :, 0:2, :])
+        nc.scalar.activation(w_bf_b[:].rearrange("p (t m j) -> p m t j", t=2, j=PACK), w_by_slot[:, :, 2:4, :], ACT.Copy)
+        w_codes = [sb.tile([P, P], U32, name="w_codes%d" % t, align_bytes=64) for t in range(PACK)]
+        w_plane = [sb.tile([P, P], U8, name="w_plane%d" % t, align_bytes=64) for t in range(PACK)]
+        for t in range(PACK):
+            src = (w_bf_a, w_bf_b)[t // 2][:, 512 * (t % 2) : 512 * (t % 2 + 1)]
+            nc.vector.quantize_mx(w_codes[t][:].bitcast(FP8X4), w_plane[t][:], src)
+
+        x_plane = sb.tile([P, S], U8, name="x_plane", align_bytes=64)
+        nc.vector.tensor_copy(x_plane[:], xs_table[:].indirect(offs_t[:]))
+
+        x_codes = sb.tile([P, S], U32, name="x_codes", tag="xs", align_bytes=64)
+        for h in range(2):
+            nc.vector.tensor_copy(
+                x_codes[:, HALF * h : HALF * (h + 1)], x_table[:].bitcast(U32).indirect(offs_t[:, 8 * h : 8 * h + 8])
+            )
+
+        def product(n_cols, codes, plane, rhs_codes, rhs_plane, tag):
+            acc = psum.tile([P, n_cols], F32, name=tag, tag=tag)
+            nc.tensor.matmul_mx(
+                out=acc[:], lhsT=codes.bitcast(FP8X4), lhsT_scale=plane,
+                rhs=rhs_codes.bitcast(FP8X4), rhs_scale=rhs_plane, start=True, stop=True,
+            )
+            return acc
+
+        y = [sb.tile([P, S], F32, name="y%d" % t) for t in range(PACK)]
+        for h in range(2):
+            cols = slice(HALF * h, HALF * (h + 1))
+            acc = product(HALF, w_codes[0][:], w_plane[0][:], x_codes[:, cols], x_plane[:, cols], "acc_a")
+            nc.scalar.activation(y[0][:, cols], acc[:], ACT.Copy)
+        for t in range(1, PACK):
+            acc = product(S, w_codes[t][:], w_plane[t][:], x_codes[:], x_plane[:], "acc_a")
+            nc.vector.tensor_copy(y[t][:], acc[:])
+
+        pair = [sb.tile([P, S], F32, name="pair%d" % t, tag="slot%d" % t, align_bytes=64) for t in range(PACK)]
+        ranked = [sb.tile([P, S], F32, name="ranked%d" % t, tag="ranked%d" % t) for t in range(PACK)]
+        dt = [sb.tile([P, S], F32, name="dt%d" % t, tag="dt%d" % t) for t in range(PACK)]
+        u = sb.tile([P, PACK * S], F32, name="u")
+
+        def fetch(t, side):
+            nc.scalar.activation(pair[t][:, W * side : W * (side + 1)], y[t][:].indirect((n1_t, n2_t)[side][:]), ACT.Copy)
+
+        def rank(t):
+            nc.vector.tensor_tensor(ranked[t][:, 0:W], pair[t][:, 0:W], pair[t][:, W:S], ALU.max)
+            nc.vector.tensor_tensor(ranked[t][:, W:S], pair[t][:, 0:W], pair[t][:, W:S], ALU.min)
+
+        def put(t, side):
+            nc.scalar.activation(dt[t][:].indirect((n1_t, n2_t)[side][:]), ranked[t][:, W * side : W * (side + 1)], ACT.Copy)
+
+        def weigh(t):
+            nc.vector.tensor_scalar(u[:, S * t : S * (t + 1)], dt[t][:], gs_t[:, t : t + 1], None, ALU.mult)
+
+        d_codes = sb.tile([P, H], U32, name="d_codes", align_bytes=64)
+
+        def pick_scales():
+            ds_picked = sb.tile([P, H], U8, name="ds_picked", tag="slot1", align_bytes=64)
+            for h in range(2):
+                nc.vector.tensor_copy(ds_picked[:, 256 * h : 256 * (h + 1)], ds_table[:].indirect(k1_t[:, 16 * h : 16 * h + 16]))
+            ds_dealt = sb.tile([P, H], U8, name="ds_dealt", align_bytes=64)
+            nc.vector.tensor_copy(
+                ds_dealt[:].rearrange("p (t a i) -> p a t i", t=PACK, i=16),
+                ds_picked[:].rearrange("p (a i t) -> p a t i", t=PACK, i=16),
+            )
+            for r in range(4):
+                nc.sync.dma_start(d_plane[r:P:32, :].bitcast(I32), ds_dealt[8 * r : P : 32, :].bitcast(I32))
+
+        def pick_words():
+            d_picked = sb.tile([P, H], U32, name="d_picked", tag="slot2", align_bytes=64)
+            for h in range(2):
+                nc.vector.tensor_copy(
+                    d_picked[:, 256 * h : 256 * (h + 1)], d_table[:].bitcast(U32).indirect(k1_t[:, 16 * h : 16 * h + 16])
+                )
+            nc.vector.tensor_copy(
+                d_codes[:].rearrange("p (t a i) -> p a t i", t=PACK, i=4),
+                d_picked[:].rearrange("p (a i t) -> p a t i", t=PACK, i=4),
+            )
+
+        fetch(0, 0)
+        fetch(0, 1)
+        rank(0)
+        fetch(1, 0)
+        fetch(1, 1)
+        rank(1)
+        pick_scales()
+        for t in range(2):
+            put(t, 0)
+            fetch(t + 2, 0)
+            put(t, 1)
+            weigh(t)
+            fetch(t + 2, 1)
+            rank(t + 2)
+            if t == 0:
+                pick_words()
+        put(2, 0)
+        put(3, 0)
+        put(2, 1)
+        weigh(2)
+        put(3, 1)
+        weigh(3)
+
+        size = [sb.tile([P, S], F32, name="size%d" % t) for t in range(PACK)]
+        neg = [sb.tile([P, HALF], F32, name="neg%d" % t) for t in range(PACK)]
+        root = [sb.tile([P, S], F32, name="root%d" % t) for t in range(PACK)]
+        others = []
+        sums = [psum.tile([P, S], F32, name="sums%d" % t, tag="acc_b") for t in range(PACK)]
+        for h in range(2):
+            cols = slice(HALF * h, HALF * (h + 1))
+            other = sb.tile([P, PACK * HALF], F32, name="other%d" % h, tag=("ranked2", "dt3")[h])
+            others.append(other)
+            for t in range(PACK):
+                nc.scalar.activation(
+                    other[:, HALF * t : HALF * (t + 1)],
+                    u[:, S * t : S * (t + 1)].indirect(n3_t[:, 8 * h : 8 * h + 8]),
+                    ACT.Copy,
+                )
+            z_bf = sb.tile([P, HALF * PACK], BF16, name="z_bf", align_bytes=64)
+            nc.vector.tensor_tensor(
+                z_bf[:].rearrange("p (c i t) -> p c t i", i=4, t=PACK),
+                u[:].rearrange("p (t j) -> p t j", t=PACK)[:, :, cols].rearrange("p t (c i) -> p c t i", i=4),
+                other[:].rearrange("p (t c i) -> p c t i", t=PACK, i=4),
+                ALU.subtract,
+            )
+            z_codes = sb.tile([P, HALF], U32, name="z_codes%d" % h, align_bytes=64)
+            z_plane = sb.tile([P, HALF], U8, name="z_plane%d" % h, align_bytes=64)
+            nc.vector.quantize_mx(z_codes[:].bitcast(FP8X4), z_plane[:], z_bf[:])
+            for t in range(PACK):
+                nc.tensor.matmul_mx(
+                    out=sums[t][:, cols], lhsT=d_codes[:, P * t : P * (t + 1)].bitcast(FP8X4), lhsT_scale=d_plane[:, P * t : P * (t + 1)],
+                    rhs=z_codes[:].bitcast(FP8X4), rhs_scale=z_plane[:], start=True, stop=True,
+                )
+            if h == 0:
+                for t in range(PACK):
+                    nc.scalar.activation(size[t][:, cols], sums[t][:, cols], ACT.Abs)
+                for t in range(PACK):
+                    nc.scalar.activation(root[t][:, cols], size[t][:, cols], ACT.Abs_reciprocal_sqrt, bias=eight[:])
+
+        late = slice(HALF, S)
+        nc.scalar.activation(size[0][:, late], sums[0][:, late], ACT.Abs)
+        for t in range(1, PACK):
+            nc.vector.tensor_scalar(neg[t][:], sums[t][:, late], -1.0, None, ALU.mult)
+        for t in range(1, PACK):
+            nc.vector.tensor_tensor(size[t][:, late], sums[t][:, late], neg[t][:], ALU.max)
+
+        out_rows = out.rearrange("(p t) j -> p t j", t=PACK)
+        nc.scalar.activation(root[0][:, late], size[0][:, late], ACT.Abs_reciprocal_sqrt, bias=eight[:])
+        for t in range(PACK):
+            if t + 1 < PACK:
+                nc.scalar.activation(root[t + 1][:, late], size[t + 1][:, late], ACT.Abs_reciprocal_sqrt, bias=eight[:])
+            picked = sb.tile([P, S], F32, name="picked%d" % t)
+            once = sb.tile([P, S], F32, name="once%d" % t)
+            res = sb.tile([P, S], F32, name="res%d" % t)
+            for h in range(2):
+                cols = slice(HALF * h, HALF * (h + 1))
+                nc.scalar.activation(picked[:, cols], root[t][:].indirect(n4_t[:, 8 * h : 8 * h + 8]), ACT.Copy)
+            for cols in ([slice(0, S)] if t + 1 < PACK else [slice(0, HALF), late]):
+                nc.vector.tensor_tensor(once[:, cols], sums[t][:, cols], picked[:, cols], ALU.mult)
+                nc.vector.tensor_tensor(res[:, cols], once[:, cols], picked[:, cols], ALU.mult)
+                nc.sync.dma_start(out_rows[:, t, cols], res[:, cols])

@@ -46,19 +46,19 @@ def tile_picked_denseorddnorm_none_p_kernel(
         d_plane = sb.tile([P, H], U8, name="d_plane", align_bytes=64)
 
         nc.vector.memset(xs_table[:].bitcast(I32), 0)
-        for q in range(4):
-            nc.gpsimd.dma_start(
-                xs_table[32 * q : 32 * q + 4, :].bitcast(I32), x_scales[0, 4 * q : 4 * q + 4, :].bitcast(I32)
-            )
         nc.vector.memset(ds_table[:].bitcast(I32), 0)
         nc.vector.memset(d_plane[:].bitcast(I32), 0)
         nc.vector.memset(eight[:], 8.0)
 
         nc.sync.dma_start(offs_t[:], offs)
         nc.sync.dma_start(w_raw[:], w1.rearrange("(p j) c -> p j c", j=PACK))
-        nc.sync.dma_start(x_table[:], x_words[0].rearrange("p n t -> p (n t)").bitcast(I32))
         nc.sync.dma_start(n1_t[:], n1)
         nc.sync.dma_start(n2_t[:], n2)
+        for q in range(4):
+            nc.sync.dma_start(
+                xs_table[32 * q : 32 * q + 4, :].bitcast(I32), x_scales[0, 4 * q : 4 * q + 4, :].bitcast(I32)
+            )
+        nc.sync.dma_start(x_table[:], x_words[0].rearrange("p n t -> p (n t)").bitcast(I32))
         nc.sync.dma_start(k1_t[:], k1)
         nc.sync.dma_start(ds_table[0:P:8, :].bitcast(I32), d_scales[0].bitcast(I32))
         nc.sync.dma_start(gs_t[:], gs.rearrange("(p t) o -> p (t o)", t=PACK))
@@ -104,27 +104,27 @@ def tile_picked_denseorddnorm_none_p_kernel(
             nc.vector.tensor_copy(y[t][:], acc[:])
 
         pair = [sb.tile([P, S], F32, name="pair%d" % t, tag="slot%d" % t, align_bytes=64) for t in range(PACK)]
-        ranked = [sb.tile([P, S], F32, name="ranked%d" % t, tag="ranked%d" % t) for t in range(PACK)]
-        dt = [sb.tile([P, S], F32, name="dt%d" % t, tag="dt%d" % t) for t in range(PACK)]
-        u = sb.tile([P, PACK * S], F32, name="u")
+        ranked, weighted, dt = {}, {}, {}
 
         def fetch(t, side):
             nc.scalar.activation(pair[t][:, W * side : W * (side + 1)], y[t][:].indirect((n1_t, n2_t)[side][:]), ACT.Copy)
 
         def rank(t):
+            ranked[t] = sb.tile([P, S], F32, name="ranked%d" % t, tag="ranked%d" % t, align_bytes=64)
             nc.vector.tensor_tensor(ranked[t][:, 0:W], pair[t][:, 0:W], pair[t][:, W:S], ALU.max)
             nc.vector.tensor_tensor(ranked[t][:, W:S], pair[t][:, 0:W], pair[t][:, W:S], ALU.min)
+            weighted[t] = sb.tile([P, S], F32, name="weighted%d" % t, tag="weighted%d" % t, align_bytes=64)
+            nc.vector.tensor_scalar(weighted[t][:], ranked[t][:], gs_t[:, t : t + 1], None, ALU.mult)
 
         def put(t, side):
-            nc.scalar.activation(dt[t][:].indirect((n1_t, n2_t)[side][:]), ranked[t][:, W * side : W * (side + 1)], ACT.Copy)
-
-        def weigh(t):
-            nc.vector.tensor_scalar(u[:, S * t : S * (t + 1)], dt[t][:], gs_t[:, t : t + 1], None, ALU.mult)
+            if side == 0:
+                dt[t] = sb.tile([P, S], F32, name="dt%d" % t, tag=("slot2", "dt1", "dt2", "dt3")[t], align_bytes=64)
+            nc.scalar.activation(dt[t][:].indirect((n1_t, n2_t)[side][:]), weighted[t][:, W * side : W * (side + 1)], ACT.Copy)
 
         d_codes = sb.tile([P, H], U32, name="d_codes", align_bytes=64)
 
         def pick_scales():
-            ds_picked = sb.tile([P, H], U8, name="ds_picked", tag="slot1", align_bytes=64)
+            ds_picked = sb.tile([P, H], U8, name="ds_picked", tag="slot3", align_bytes=64)
             for h in range(2):
                 nc.vector.tensor_copy(ds_picked[:, 256 * h : 256 * (h + 1)], ds_table[:].indirect(k1_t[:, 16 * h : 16 * h + 16]))
             ds_dealt = sb.tile([P, H], U8, name="ds_dealt", align_bytes=64)
@@ -132,11 +132,13 @@ def tile_picked_denseorddnorm_none_p_kernel(
                 ds_dealt[:].rearrange("p (t a i) -> p a t i", t=PACK, i=16),
                 ds_picked[:].rearrange("p (a i t) -> p a t i", t=PACK, i=16),
             )
-            for r in range(4):
-                nc.sync.dma_start(d_plane[r:P:32, :].bitcast(I32), ds_dealt[8 * r : P : 32, :].bitcast(I32))
+            for q in range(4):
+                nc.sync.dma_start(
+                    d_plane[32 * q : 32 * q + 4, :].bitcast(I32), ds_dealt[32 * q : 32 * q + 32 : 8, :].bitcast(I32)
+                )
 
         def pick_words():
-            d_picked = sb.tile([P, H], U32, name="d_picked", tag="slot2", align_bytes=64)
+            d_picked = sb.tile([P, H], U32, name="d_picked", tag="slot3", align_bytes=64)
             for h in range(2):
                 nc.vector.tensor_copy(
                     d_picked[:, 256 * h : 256 * (h + 1)], d_table[:].bitcast(U32).indirect(k1_t[:, 16 * h : 16 * h + 16])
@@ -146,84 +148,90 @@ def tile_picked_denseorddnorm_none_p_kernel(
                 d_picked[:].rearrange("p (a i t) -> p a t i", t=PACK, i=4),
             )
 
-        fetch(0, 0)
-        fetch(0, 1)
-        rank(0)
-        fetch(1, 0)
-        fetch(1, 1)
-        rank(1)
+        for t in range(PACK):
+            fetch(t, 0)
+            fetch(t, 1)
+            rank(t)
         pick_scales()
-        for t in range(2):
-            put(t, 0)
-            fetch(t + 2, 0)
-            put(t, 1)
-            weigh(t)
-            fetch(t + 2, 1)
-            rank(t + 2)
-            if t == 0:
-                pick_words()
-        put(2, 0)
-        put(3, 0)
-        put(2, 1)
-        weigh(2)
-        put(3, 1)
-        weigh(3)
+        pick_words()
+        for t in range(0, PACK, 2):
+            for side in range(2):
+                put(t, side)
+                put(t + 1, side)
 
         size = [sb.tile([P, S], F32, name="size%d" % t) for t in range(PACK)]
-        neg = [sb.tile([P, HALF], F32, name="neg%d" % t) for t in range(PACK)]
+        neg = [sb.tile([P, S], F32, name="neg%d" % t) for t in range(PACK)]
         root = [sb.tile([P, S], F32, name="root%d" % t) for t in range(PACK)]
-        others = []
+        inverse = [sb.tile([P, S], F32, name="inverse%d" % t) for t in range(PACK)]
         sums = [psum.tile([P, S], F32, name="sums%d" % t, tag="acc_b") for t in range(PACK)]
-        for h in range(2):
-            cols = slice(HALF * h, HALF * (h + 1))
-            other = sb.tile([P, PACK * HALF], F32, name="other%d" % h, tag=("ranked2", "dt3")[h])
-            others.append(other)
+        early, late = slice(0, HALF), slice(HALF, S)
+
+        def magnitude(t, cols):
+            nc.scalar.activation(size[t][:, cols], sums[t][:, cols], ACT.Abs)
+
+        def inverse_root(t, cols):
+            nc.scalar.activation(root[t][:, cols], size[t][:, cols], ACT.Abs_reciprocal_sqrt, bias=eight[:])
+
+        pieces = [(0, 128, "z_bf_a"), (128, 128, "z_bf_a")]
+        others = sb.tile([P, PACK * S], F32, name="others", tag="slot3", align_bytes=64)
+        for n, (first, width, z_tag) in enumerate(pieces):
+            cols = slice(first, first + width)
+            other = others[:, PACK * first : PACK * (first + width)]
+            diff = sb.tile([P, PACK * width], F32, name="diff%d" % n)
             for t in range(PACK):
                 nc.scalar.activation(
-                    other[:, HALF * t : HALF * (t + 1)],
-                    u[:, S * t : S * (t + 1)].indirect(n3_t[:, 8 * h : 8 * h + 8]),
+                    other[:, width * t : width * (t + 1)],
+                    dt[t][:].indirect(n3_t[:, first // 16 : (first + width) // 16]),
                     ACT.Copy,
                 )
-            z_bf = sb.tile([P, HALF * PACK], BF16, name="z_bf", align_bytes=64)
-            nc.vector.tensor_tensor(
+                nc.vector.tensor_tensor(
+                    diff[:, width * t : width * (t + 1)], dt[t][:, cols], other[:, width * t : width * (t + 1)], ALU.subtract
+                )
+            z_bf = sb.tile([P, width * PACK], BF16, name="z_bf%d" % n, tag=z_tag, align_bytes=64)
+            nc.vector.tensor_copy(
                 z_bf[:].rearrange("p (c i t) -> p c t i", i=4, t=PACK),
-                u[:].rearrange("p (t j) -> p t j", t=PACK)[:, :, cols].rearrange("p t (c i) -> p c t i", i=4),
-                other[:].rearrange("p (t c i) -> p c t i", t=PACK, i=4),
-                ALU.subtract,
+                diff[:].rearrange("p (t c i) -> p c t i", t=PACK, i=4),
             )
-            z_codes = sb.tile([P, HALF], U32, name="z_codes%d" % h, align_bytes=64)
-            z_plane = sb.tile([P, HALF], U8, name="z_plane%d" % h, align_bytes=64)
+            z_codes = sb.tile([P, width], U32, name="z_codes%d" % n, align_bytes=64)
+            z_plane = sb.tile([P, width], U8, name="z_plane%d" % n, align_bytes=64)
             nc.vector.quantize_mx(z_codes[:].bitcast(FP8X4), z_plane[:], z_bf[:])
             for t in range(PACK):
                 nc.tensor.matmul_mx(
                     out=sums[t][:, cols], lhsT=d_codes[:, P * t : P * (t + 1)].bitcast(FP8X4), lhsT_scale=d_plane[:, P * t : P * (t + 1)],
                     rhs=z_codes[:].bitcast(FP8X4), rhs_scale=z_plane[:], start=True, stop=True,
                 )
-            if h == 0:
+            if n == 0:
                 for t in range(PACK):
-                    nc.scalar.activation(size[t][:, cols], sums[t][:, cols], ACT.Abs)
+                    magnitude(t, early)
                 for t in range(PACK):
-                    nc.scalar.activation(root[t][:, cols], size[t][:, cols], ACT.Abs_reciprocal_sqrt, bias=eight[:])
+                    inverse_root(t, early)
 
-        late = slice(HALF, S)
-        nc.scalar.activation(size[0][:, late], sums[0][:, late], ACT.Abs)
-        for t in range(1, PACK):
-            nc.vector.tensor_scalar(neg[t][:], sums[t][:, late], -1.0, None, ALU.mult)
-        for t in range(1, PACK):
-            nc.vector.tensor_tensor(size[t][:, late], sums[t][:, late], neg[t][:], ALU.max)
+        for t in range(2):
+            magnitude(t, late)
+        for t in range(2):
+            inverse_root(t, late)
+        for t in range(2, PACK):
+            nc.vector.tensor_scalar(neg[t][:, late], sums[t][:, late], -1.0, None, ALU.mult)
+        nc.vector.tensor_tensor(size[2][:, late], sums[2][:, late], neg[2][:, late], ALU.max)
+        nc.vector.tensor_tensor(inverse[1][:], root[1][:], root[1][:], ALU.mult)
+        nc.vector.tensor_tensor(size[3][:, late], sums[3][:, late], neg[3][:, late], ALU.max)
 
         out_rows = out.rearrange("(p t) j -> p t j", t=PACK)
-        nc.scalar.activation(root[0][:, late], size[0][:, late], ACT.Abs_reciprocal_sqrt, bias=eight[:])
+        picks = []
         for t in range(PACK):
-            if t + 1 < PACK:
-                nc.scalar.activation(root[t + 1][:, late], size[t + 1][:, late], ACT.Abs_reciprocal_sqrt, bias=eight[:])
             picked = sb.tile([P, S], F32, name="picked%d" % t)
-            once = sb.tile([P, S], F32, name="once%d" % t)
+            picks.append(picked)
             res = sb.tile([P, S], F32, name="res%d" % t)
+            window = root[0] if t == 0 else inverse[t]
             for h in range(2):
                 cols = slice(HALF * h, HALF * (h + 1))
-                nc.scalar.activation(picked[:, cols], root[t][:].indirect(n4_t[:, 8 * h : 8 * h + 8]), ACT.Copy)
-            for cols in ([slice(0, S)] if t + 1 < PACK else [slice(0, HALF), late]):
-                nc.vector.tensor_tensor(once[:, cols], sums[t][:, cols], picked[:, cols], ALU.mult)
-                nc.vector.tensor_tensor(res[:, cols], once[:, cols], picked[:, cols], ALU.mult)
+                nc.scalar.activation(picked[:, cols], window[:].indirect(n4_t[:, 8 * h : 8 * h + 8]), ACT.Copy)
+            if t + 2 < PACK:
+                inverse_root(t + 2, late)
+                nc.vector.tensor_tensor(inverse[t + 2][:], root[t + 2][:], root[t + 2][:], ALU.mult)
+            if t == 0:
+                nc.vector.tensor_tensor(inverse[0][:], picked[:], picked[:], ALU.mult)
+                picked = inverse[0]
+            for cols in ([slice(0, S)] if t + 1 < PACK else [early, late]):
+                nc.vector.tensor_tensor(res[:, cols], sums[t][:, cols], picked[:, cols], ALU.mult)
                 nc.sync.dma_start(out_rows[:, t, cols], res[:, cols])

@@ -50,6 +50,8 @@ def tile_picked_denseorddnorm_none_p_kernel(
         nc.vector.memset(d_plane[:].bitcast(I32), 0)
         nc.vector.memset(eight[:], 8.0)
 
+        warm = sb.tile([P, 1], F32, name="warm")
+        nc.scalar.activation(warm[:], eight[:], ACT.Abs_reciprocal_sqrt, bias=eight[:])
         nc.sync.dma_start(offs_t[:], offs)
         nc.sync.dma_start(w_raw[:], w1.rearrange("(p j) c -> p j c", j=PACK))
         nc.sync.dma_start(n1_t[:], n1)

from contextlib import ExitStack

import concourse.mybir as mybir

K, T, S, H, W, G = 512, 2048, 256, 512, 128, 2048
FLOPS = 2 * K * H * S + 2 * K * H * S

F32 = mybir.dt.float32
BF16 = mybir.dt.bfloat16
I32 = mybir.dt.int32
U32 = mybir.dt.uint32
U16 = mybir.dt.uint16
U8 = mybir.dt.uint8
FP8X4 = mybir.dt.float8_e4m3fn_x4
ALU = mybir.AluOpType
ACT = mybir.ActivationFunctionType

P = 128
PACK = 4
HALF = S // 2


def tile_picked_denseorddnorm_none_p_kernel(
    tc, x_words, x_scales, w1, gs, d_words, d_scales, offs, n1, n2, n3, k1, n4, out
):
    nc = tc.nc
    with ExitStack() as ctx:
        lists = ctx.enter_context(tc.tile_pool(name="lists", bufs=1))
        sb = ctx.enter_context(tc.tile_pool(name="sb", bufs=1))
        psum = ctx.enter_context(tc.psum_pool(name="psum", bufs=4))

        offs_t = lists.tile([P, S // 16], U16, name="offs_t")
        n1_t = lists.tile([P, W // 16], U16, name="n1_t")
        n2_t = lists.tile([P, W // 16], U16, name="n2_t")
        n3_t = lists.tile([P, S // 16], U16, name="n3_t")
        k1_t = lists.tile([P, H // 16], U16, name="k1_t")
        n4_t = lists.tile([P, S // 16], U16, name="n4_t")

        x_table = sb.tile([P, T], I32, name="x_table", align_bytes=64)
        xs_table = sb.tile([P, T], U8, name="xs_table", tag="xs", align_bytes=64)
        d_table = sb.tile([P, G], I32, name="d_table", align_bytes=64)
        ds_table = sb.tile([P, G], U8, name="ds_table", align_bytes=64)
        w_raw = sb.tile([P, PACK, H], F32, name="w_raw", align_bytes=64)
        gs_t = sb.tile([P, PACK], F32, name="gs_t")
        eight = sb.tile([P, 1], F32, name="eight")
        d_plane = sb.tile([P, H], U8, name="d_plane", align_bytes=64)

        nc.vector.memset(xs_table[:].bitcast(I32), 0)
        nc.vector.memset(ds_table[:].bitcast(I32), 0)
        nc.vector.memset(d_plane[:].bitcast(I32), 0)
        nc.vector.memset(eight[:], 8.0)

        warm = sb.tile([P, 1], F32, name="warm")
        nc.scalar.activation(warm[:], eight[:], ACT.Abs_reciprocal_sqrt, bias=eight[:])
        nc.sync.dma_start(offs_t[:], offs)
        nc.sync.dma_start(w_raw[:], w1.rearrange("(p j) c -> p j c", j=PACK))
        nc.sync.dma_start(n1_t[:], n1)
        nc.sync.dma_start(n2_t[:], n2)
        for q in range(4):
            nc.sync.dma_start(
                xs_table[32 * q : 32 * q + 4, :].bitcast(I32), x_scales[0, 4 * q : 4 * q + 4, :].bitcast(I32)
            )
        nc.sync.dma_start(x_table[:], x_words[0].rearrange("p n t -> p (n t)").bitcast(I32))
        nc.sync.dma_start(k1_t[:], k1)
        nc.sync.dma_start(ds_table[0:P:8, :].bitcast(I32), d_scales[0].bitcast(I32))
        nc.sync.dma_start(gs_t[:], gs.rearrange("(p t) o -> p (t o)", t=PACK))
        nc.sync.dma_start(d_table[:], d_words[0].rearrange("p n t -> p (n t)").bitcast(I32))
        nc.sync.dma_start(n3_t[:], n3)
        nc.sync.dma_start(n4_t[:], n4)

        w_by_slot = w_raw[:].rearrange("p j (m t) -> p m t j", t=PACK)
        w_bf_a = sb.tile([P, 2 * P * PACK], BF16, name="w_bf_a", align_bytes=64)
        w_bf_b = sb.tile([P, 2 * P * PACK], BF16, name="w_bf_b", align_bytes=64)
        nc.vector.tensor_copy(w_bf_a[:].rearrange("p (t m j) -> p m t j", t=2, j=PACK), w_by_slot[:, :, 0:2, :])
        nc.scalar.activation(w_bf_b[:].rearrange("p (t m j) -> p m t j", t=2, j=PACK), w_by_slot[:, :, 2:4, :], ACT.Copy)
        w_codes = [sb.tile([P, P], U32, name="w_codes%d" % t, align_bytes=64) for t in range(PACK)]
        w_plane = [sb.tile([P, P], U8, name="w_plane%d" % t, align_bytes=64) for t in range(PACK)]
        for t in range(PACK):
            src = (w_bf_a, w_bf_b)[t // 2][:, 512 * (t % 2) : 512 * (t % 2 + 1)]
            nc.vector.quantize_mx(w_codes[t][:].bitcast(FP8X4), w_plane[t][:], src)

        x_plane = sb.tile([P, S], U8, name="x_plane", align_bytes=64)
        nc.vector.tensor_copy(x_plane[:], xs_table[:].indirect(offs_t[:]))

        x_codes = sb.tile([P, S], U32, name="x_codes", tag="xs", align_bytes=64)
        for h in range(2):
            nc.vector.tensor_copy(
                x_codes[:, HALF * h : HALF * (h + 1)], x_table[:].bitcast(U32).indirect(offs_t[:, 8 * h : 8 * h + 8])
            )

        def product(n_cols, codes, plane, rhs_codes, rhs_plane, tag):
            acc = psum.tile([P, n_cols], F32, name=tag, tag=tag)
            nc.tensor.matmul_mx(
                out=acc[:], lhsT=codes.bitcast(FP8X4), lhsT_scale=plane,
                rhs=rhs_codes.bitcast(FP8X4), rhs_scale=rhs_plane, start=True, stop=True,
            )
            return acc

        y = [sb.tile([P, S], F32, name="y%d" % t) for t in range(PACK)]
        for h in range(2):
            cols = slice(HALF * h, HALF * (h + 1))
            acc = product(HALF, w_codes[0][:], w_plane[0][:], x_codes[:, cols], x_plane[:, cols], "acc_a")
            nc.scalar.activation(y[0][:, cols], acc[:], ACT.Copy)
        for t in range(1, PACK):
            acc = product(S, w_codes[t][:], w_plane[t][:], x_codes[:], x_plane[:], "acc_a")
            nc.vector.tensor_copy(y[t][:], acc[:])

        pair = [sb.tile([P, S], F32, name="pair%d" % t, tag="slot%d" % t, align_bytes=64) for t in range(PACK)]
        ranked, weighted, dt = {}, {}, {}

        def fetch(t, side):
            nc.scalar.activation(pair[t][:, W * side : W * (side + 1)], y[t][:].indirect((n1_t, n2_t)[side][:]), ACT.Copy)

        def rank(t):
            ranked[t] = sb.tile([P, S], F32, name="ranked%d" % t, tag="ranked%d" % t, align_bytes=64)
            nc.vector.tensor_tensor(ranked[t][:, 0:W], pair[t][:, 0:W], pair[t][:, W:S], ALU.max)
            nc.vector.tensor_tensor(ranked[t][:, W:S], pair[t][:, 0:W], pair[t][:, W:S], ALU.min)
            weighted[t] = sb.tile([P, S], F32, name="weighted%d" % t, tag="weighted%d" % t, align_bytes=64)
            nc.vector.tensor_scalar(weighted[t][:], ranked[t][:], gs_t[:, t : t + 1], None, ALU.mult)

        def put(t, side):
            if side == 0:
                dt[t] = sb.tile([P, S], F32, name="dt%d" % t, tag=("slot2", "dt1", "dt2", "dt3")[t], align_bytes=64)
            nc.scalar.activation(dt[t][:].indirect((n1_t, n2_t)[side][:]), weighted[t][:, W * side : W * (side + 1)], ACT.Copy)

        d_codes = sb.tile([P, H], U32, name="d_codes", align_bytes=64)

        def pick_scales():
            ds_picked = sb.tile([P, H], U8, name="ds_picked", tag="slot3", align_bytes=64)
            for h in range(2):
                nc.vector.tensor_copy(ds_picked[:, 256 * h : 256 * (h + 1)], ds_table[:].indirect(k1_t[:, 16 * h : 16 * h + 16]))
            ds_dealt = sb.tile([P, H], U8, name="ds_dealt", align_bytes=64)
            nc.vector.tensor_copy(
                ds_dealt[:].rearrange("p (t a i) -> p a t i", t=PACK, i=16),
                ds_picked[:].rearrange("p (a i t) -> p a t i", t=PACK, i=16),
            )
            for q in range(4):
                nc.sync.dma_start(
                    d_plane[32 * q : 32 * q + 4, :].bitcast(I32), ds_dealt[32 * q : 32 * q + 32 : 8, :].bitcast(I32)
                )

        def pick_words():
            d_picked = sb.tile([P, H], U32, name="d_picked", tag="slot3", align_bytes=64)
            for h in range(2):
                nc.vector.tensor_copy(
                    d_picked[:, 256 * h : 256 * (h + 1)], d_table[:].bitcast(U32).indirect(k1_t[:, 16 * h : 16 * h + 16])
                )
            nc.vector.tensor_copy(
                d_codes[:].rearrange("p (t a i) -> p a t i", t=PACK, i=4),
                d_picked[:].rearrange("p (a i t) -> p a t i", t=PACK, i=4),
            )

        for t in range(PACK):
            fetch(t, 0)
            fetch(t, 1)
            rank(t)
        pick_scales()
        pick_words()
        for t in range(0, PACK, 2):
            for side in range(2):
                put(t, side)
                put(t + 1, side)

        size = [sb.tile([P, S], F32, name="size%d" % t) for t in range(PACK)]
        neg = [sb.tile([P, S], F32, name="neg%d" % t) for t in range(PACK)]
        root = [sb.tile([P, S], F32, name="root%d" % t) for t in range(PACK)]
        inverse = [sb.tile([P, S], F32, name="inverse%d" % t) for t in range(PACK)]
        sums = [psum.tile([P, S], F32, name="sums%d" % t, tag="acc_b") for t in range(PACK)]
        early, late = slice(0, HALF), slice(HALF, S)

        def magnitude(t, cols):
            nc.scalar.activation(size[t][:, cols], sums[t][:, cols], ACT.Abs)

        def inverse_root(t, cols):
            nc.scalar.activation(root[t][:, cols], size[t][:, cols], ACT.Abs_reciprocal_sqrt, bias=eight[:])

        pieces = [(0, 128, "z_bf_a"), (128, 128, "z_bf_a")]
        others = sb.tile([P, PACK * S], F32, name="others", tag="slot3", align_bytes=64)
        for n, (first, width, z_tag) in enumerate(pieces):
            cols = slice(first, first + width)
            other = others[:, PACK * first : PACK * (first + width)]
            diff = sb.tile([P, PACK * width], F32, name="diff%d" % n)
            for t in range(PACK):
                nc.scalar.activation(
                    other[:, width * t : width * (t + 1)],
                    dt[t][:].indirect(n3_t[:, first // 16 : (first + width) // 16]),
                    ACT.Copy,
                )
                nc.vector.tensor_tensor(
                    diff[:, width * t : width * (t + 1)], dt[t][:, cols], other[:, width * t : width * (t + 1)], ALU.subtract
                )
            z_bf = sb.tile([P, width * PACK], BF16, name="z_bf%d" % n, tag=z_tag, align_bytes=64)
            nc.vector.tensor_copy(
                z_bf[:].rearrange("p (c i t) -> p c t i", i=4, t=PACK),
                diff[:].rearrange("p (t c i) -> p c t i", t=PACK, i=4),
            )
            z_codes = sb.tile([P, width], U32, name="z_codes%d" % n, align_bytes=64)
            z_plane = sb.tile([P, width], U8, name="z_plane%d" % n, align_bytes=64)
            nc.vector.quantize_mx(z_codes[:].bitcast(FP8X4), z_plane[:], z_bf[:])
            for t in range(PACK):
                nc.tensor.matmul_mx(
                    out=sums[t][:, cols], lhsT=d_codes[:, P * t : P * (t + 1)].bitcast(FP8X4), lhsT_scale=d_plane[:, P * t : P * (t + 1)],
                    rhs=z_codes[:].bitcast(FP8X4), rhs_scale=z_plane[:], start=True, stop=True,
                )
            if n == 0:
                for t in range(PACK):
                    magnitude(t, early)
                for t in range(PACK):
                    inverse_root(t, early)

        for t in range(2):
            magnitude(t, late)
        for t in range(2):
            inverse_root(t, late)
        for t in range(2, PACK):
            nc.vector.tensor_scalar(neg[t][:, late], sums[t][:, late], -1.0, None, ALU.mult)
        nc.vector.tensor_tensor(size[2][:, late], sums[2][:, late], neg[2][:, late], ALU.max)
        nc.vector.tensor_tensor(inverse[1][:], root[1][:], root[1][:], ALU.mult)
        nc.vector.tensor_tensor(size[3][:, late], sums[3][:, late], neg[3][:, late], ALU.max)

        out_rows = out.rearrange("(p t) j -> p t j", t=PACK)
        picks = []
        for t in range(PACK):
            picked = sb.tile([P, S], F32, name="picked%d" % t)
            picks.append(picked)
            res = sb.tile([P, S], F32, name="res%d" % t)
            window = root[0] if t == 0 else inverse[t]
            for h in range(2):
                cols = slice(HALF * h, HALF * (h + 1))
                nc.scalar.activation(picked[:, cols], window[:].indirect(n4_t[:, 8 * h : 8 * h + 8]), ACT.Copy)
            if t + 2 < PACK:
                inverse_root(t + 2, late)
                nc.vector.tensor_tensor(inverse[t + 2][:], root[t + 2][:], root[t + 2][:], ALU.mult)
            if t == 0:
                nc.vector.tensor_tensor(inverse[0][:], picked[:], picked[:], ALU.mult)
                picked = inverse[0]
            for cols in ([slice(0, S)] if t + 1 < PACK else [early, late]):
                nc.vector.tensor_tensor(res[:, cols], sums[t][:, cols], picked[:, cols], ALU.mult)
                nc.sync.dma_start(out_rows[:, t, cols], res[:, cols])
